import numpy as np
import ml_dtypes


def mxq(x, axis, fmt="e4m3"):
    dtype, down = {"e4m3": (ml_dtypes.float8_e4m3fn, 7), "e5m2": (ml_dtypes.float8_e5m2, 14)}[fmt]
    v = np.moveaxis(np.asarray(x, np.float32).astype(ml_dtypes.bfloat16).astype(np.float64), axis, -1)
    blocks = v.reshape(v.shape[:-1] + (-1, 32))
    amax = np.abs(blocks).max(-1, keepdims=True)
    byte = np.maximum(np.where(amax > 0, np.frexp(amax)[1] - 1 + 127, 0) - down, 1)
    scale = np.exp2(byte - 127.0)
    codes = (blocks / scale).astype(np.float32).astype(dtype).astype(np.float64)
    return np.moveaxis((codes * scale).reshape(v.shape), -1, axis)


WIDE = False


def mx_kscale(k):
    if not WIDE:
        return np.ones(k)
    levels = np.array([30, -30])
    if k % 512:
        return np.exp2(np.random.permutation(np.resize(levels, k // 32))).repeat(32)
    a = np.empty((k // 512, 16))
    for p in range(k // 512):
        a[p, :8] = np.random.permutation(np.resize(levels, 8))
        for g in range(8):
            far = levels[np.abs(levels - a[p, g]) >= 10]
            a[p, g + 8] = far[np.random.randint(len(far))]
    return np.exp2(a.ravel()).repeat(32)


def f64(x):
    return np.asarray(x).astype(np.float64)


def striped(idx):
    return np.tile(np.asarray(idx).reshape(-1, 16).T, (8, 1)).astype(np.uint16)


def unstriped(offs):
    return offs[:16].T.reshape(-1).astype(np.int64)


E2M1 = np.array([0.0, 0.5, 1.0, 1.5, 2.0, 3.0, 4.0, 6.0, -0.0, -0.5, -1.0, -1.5, -2.0, -3.0, -4.0, -6.0])


def pack_weight(w, fmt):
    k, n = w.shape
    w = f64(np.asarray(w, np.float32).astype(ml_dtypes.bfloat16)).reshape(k // 32, 32, n)
    amax = np.abs(w).max(1)
    if fmt in ("e4m3", "e5m2"):
        byte = np.frexp(amax)[1] - 1 + 127 - (7 if fmt == "e4m3" else 14)
    else:
        mant, ex = np.frexp(amax / 6.0)
        byte = np.where(mant > 0.5, ex, ex - 1) + 127
    byte = np.clip(np.where(amax > 0, byte, 1), 1, 254)
    scaled = (w * np.exp2(127.0 - byte)[:, None, :]).reshape(k, n).astype(np.float32)
    by_word = np.ascontiguousarray(scaled.reshape(k // 512, 128, 4, n).transpose(0, 1, 3, 2))
    if fmt in ("e4m3", "e5m2"):
        words = by_word.astype(ml_dtypes.float8_e4m3fn if fmt == "e4m3" else ml_dtypes.float8_e5m2).view(np.uint8)
    else:
        c = by_word.astype(ml_dtypes.float4_e2m1fn).view(np.uint8) & 0xF
        words = (c[..., 0::2] | (c[..., 1::2] << 4)).reshape(k // 512, 128, 2 * n)
    return np.ascontiguousarray(words), np.ascontiguousarray(byte.astype(np.uint8).reshape(k // 512, 16, n))


def unpack_weight(words, scales, fmt):
    g, _, n = scales.shape
    words = np.ascontiguousarray(words).reshape(g, 128, n, -1)
    if fmt in ("e4m3", "e5m2"):
        vals = words.view(ml_dtypes.float8_e4m3fn if fmt == "e4m3" else ml_dtypes.float8_e5m2).astype(np.float64)
    else:
        nib = np.empty((g, 128, n, 4), np.uint8)
        nib[..., 0::2] = words & 0xF
        nib[..., 1::2] = words >> 4
        vals = E2M1[nib]
    vals = vals * np.repeat(np.exp2(scales.astype(np.float64) - 127.0), 8, axis=1)[..., None]
    return vals.transpose(0, 1, 3, 2).reshape(g * 512, n)


K, T, Z, J, R, N, O = 512, 1024, 1024, 256, 512, 256, 128


def setup_inputs():
    n = np.random.standard_normal
    idx = np.random.permutation(T)[:J]
    idx2 = np.random.permutation(Z)[:J]
    idx3 = np.random.permutation(J)[:O]
    idx4 = np.random.permutation(J)[:O]
    fk = mx_kscale(K)
    fr = mx_kscale(R)
    xtp = pack_weight(n((K, T)) / fk[:, None], "e2m1")
    xop = pack_weight(n((K, Z)) / fk[:, None], "e4m3")
    wp = pack_weight(n((K, R)) * 1 / np.sqrt(K) * fk[:, None] * fr, "e4m3")
    wbp = pack_weight(n((R, N)) * 1 / np.sqrt(R) / fr[:, None], "e2m1")
    wcp = pack_weight(n((R, N)) * 1 / np.sqrt(R) / fr[:, None], "e5m2")
    return {
        "xt_words": xtp[0],
        "xt_scales": xtp[1],
        "xo_words": xop[0],
        "xo_scales": xop[1],
        "w_words": wp[0],
        "w_scales": wp[1],
        "wb_words": wbp[0],
        "wb_scales": wbp[1],
        "wc_words": wcp[0],
        "wc_scales": wcp[1],
        "so": (np.random.uniform(0.5, 1.6, (N, 1))).astype(np.float32),
        "sp": (np.random.uniform(0.5, 1.6, (N, 1))).astype(np.float32),
        "offs": striped(idx),
        "offs2": striped(idx2),
        "offs3": striped(idx3),
        "offs4": striped(idx4),
    }


def reference(xt_words, xt_scales, xo_words, xo_scales, w_words, w_scales, wb_words, wb_scales, wc_words, wc_scales, so, sp, offs, offs2, offs3, offs4):
    idx = unstriped(offs)
    idx2 = unstriped(offs2)
    idx3 = unstriped(offs3)
    idx4 = unstriped(offs4)
    xtu = unpack_weight(xt_words, xt_scales, "e2m1")
    xou = unpack_weight(xo_words, xo_scales, "e4m3")
    wu = unpack_weight(w_words, w_scales, "e4m3")
    wbu = unpack_weight(wb_words, wb_scales, "e2m1")
    wcu = unpack_weight(wc_words, wc_scales, "e5m2")
    xtidxg = xtu[:, idx]
    a = wu.T @ xtidxg
    xoidx2g = xou[:, idx2]
    b = wu.T @ xoidx2g
    hid = np.maximum(a, b)
    hidq = mxq(hid, 0, "e5m2")
    p = wbu.T @ hidq
    q = wcu.T @ hidq
    y = np.maximum(p[:, idx3] * f64(so), q[:, idx4] * f64(sp))
    return y

@@ -1,0 +1,170 @@
+from contextlib import ExitStack
+
+import concourse.mybir as mybir
+
+K, T, Z, J, R, N, O = 512, 1024, 1024, 256, 512, 256, 128
+FLOPS = 2 * (2 * K * R * J + 2 * R * N * J)
+
+F32 = mybir.dt.float32
+BF16 = mybir.dt.bfloat16
+I32 = mybir.dt.int32
+U32 = mybir.dt.uint32
+U16 = mybir.dt.uint16
+U8 = mybir.dt.uint8
+E4M3 = mybir.dt.float8_e4m3fn_x4
+E5M2 = mybir.dt.float8_e5m2_x4
+E2M1 = mybir.dt.float4_e2m1fn_x4
+COPY = mybir.ActivationFunctionType.Copy
+MAX = mybir.AluOpType.max
+
+P = 128
+H = 128
+XO_ROW = 4
+
+
+def tile_list_outcomesweighed_oneforboth_kernel(
+    tc, xt_words, xt_scales, xo_words, xo_scales, w_words, w_scales, wb_words, wb_scales,
+    wc_words, wc_scales, so, sp, offs, offs2, offs3, offs4, out,
+):
+    nc = tc.nc
+    with ExitStack() as ctx:
+        sb = ctx.enter_context(tc.tile_pool(name="sb", bufs=1))
+        ps = ctx.enter_context(tc.psum_pool(name="ps", bufs=1))
+
+        def sbuf(name, shape, dtype, tag=None):
+            return sb.tile(shape, dtype, name=name, tag=tag or name, align_bytes=64)
+
+        l1 = sbuf("l1", [P, J // 16], U16)
+        l2 = sbuf("l2", [P, J // 16], U16)
+        l3 = sbuf("l3", [P, O // 16], U16)
+        l4 = sbuf("l4", [P, O // 16], U16)
+        xt_tab = sbuf("xt_tab", [P, T], U16)
+        xo_tab = sbuf("xo_tab", [P, Z], U32)
+        w_raw = sbuf("w_raw", [P, R], U32)
+        xt_stage = sbuf("xt_stage", [P, 2, T], U8)
+        xt_plane = sbuf("xt_plane", [P, T], U8)
+        xo_plane = sbuf("xo_plane", [P, Z], U8)
+        w_stage = sbuf("w_stage", [P, 2, R], U8)
+        bc_stage = sbuf("bc_stage", [P, 2, 2 * N], U8)
+        wb_tab = sbuf("wb_tab", [P, N // 2], U32)
+        wc_tab = sbuf("wc_tab", [P, N], U32)
+
+        def flat32(t):
+            return t[:].rearrange("p a c -> p (a c)").bitcast(I32)
+
+        nc.vector.memset(flat32(w_stage)[0:64], 0)
+        nc.vector.memset(flat32(xt_stage)[64:128], 0)
+        nc.vector.memset(xo_plane[:].bitcast(I32), 0)
+        nc.vector.memset(flat32(bc_stage)[0:64], 0)
+
+        def paired(scales):
+            return scales[0].bitcast(I32).rearrange("(a b r) c -> b r a c", a=2, b=2)
+
+        def words32(words):
+            return words[0].rearrange("p n t -> p (n t)").bitcast(I32)
+
+        nc.sync.dma_start(l1[:], offs)
+        nc.sync.dma_start(xt_tab[:].bitcast(I32), xt_words[0].bitcast(I32))
+        nc.sync.dma_start(w_raw[:].bitcast(I32), words32(w_words))
+        nc.scalar.dma_start(w_stage[0:4].bitcast(I32), paired(w_scales)[0])
+        nc.scalar.dma_start(w_stage[32:36].bitcast(I32), paired(w_scales)[1])
+        nc.scalar.dma_start(xt_stage[64:68].bitcast(I32), paired(xt_scales)[0])
+        nc.scalar.dma_start(xt_stage[96:100].bitcast(I32), paired(xt_scales)[1])
+        nc.sync.dma_start(xo_tab[:].bitcast(I32), words32(xo_words))
+        nc.sync.dma_start(l2[:], offs2)
+        nc.sync.dma_start(xo_plane[4:8].bitcast(I32), xo_scales[0, 0:4].bitcast(I32))
+        nc.sync.dma_start(xo_plane[36:40].bitcast(I32), xo_scales[0, 4:8].bitcast(I32))
+        nc.sync.dma_start(xo_plane[68:72].bitcast(I32), xo_scales[0, 8:12].bitcast(I32))
+        nc.sync.dma_start(xo_plane[100:104].bitcast(I32), xo_scales[0, 12:16].bitcast(I32))
+
+        nc.vector.tensor_copy(w_stage[64:128, 0, :].bitcast(I32), w_stage[0:64, 1, :].bitcast(I32))
+        w_plane = sbuf("w_plane", [P, R], U8)
+        nc.gpsimd.tensor_copy(
+            w_plane[:].rearrange("p (t m) -> p t m", t=4),
+            w_stage[:, 0, :].rearrange("p (m t) -> p t m", t=4),
+        )
+        w_tab = sbuf("w_tab", [P, R], U32)
+        nc.scalar.copy(
+            w_tab[:].rearrange("p (t c i) -> p c t i", t=4, i=4),
+            w_raw[:].rearrange("p (c i t) -> p c t i", t=4, i=4),
+        )
+        nc.vector.tensor_copy(xt_plane[64:128].bitcast(I32), xt_stage[64:128, 1, :].bitcast(I32))
+        nc.vector.tensor_copy(xt_plane[0:64].bitcast(I32), xt_stage[64:128, 0, :].bitcast(I32))
+
+        for b in range(2):
+            nc.sync.dma_start(bc_stage[32 * b : 32 * b + 4, :, 0:N].bitcast(I32), paired(wb_scales)[b])
+            nc.sync.dma_start(bc_stage[32 * b : 32 * b + 4, :, N : 2 * N].bitcast(I32), paired(wc_scales)[b])
+        nc.sync.dma_start(wb_tab[:].bitcast(I32), wb_words[0].bitcast(I32))
+        nc.sync.dma_start(wc_tab[:].bitcast(I32), words32(wc_words))
+        nc.sync.dma_start(l3[:], offs3)
+        nc.sync.dma_start(l4[:], offs4)
+        weights = sbuf("weights", [P, 2, 8], F32)
+        with nc.allow_non_contiguous_dma(reason="one float32 a partition and row block"):
+            nc.sync.dma_start(weights[:, 0, 0:2], so.rearrange("(h p) o -> p (h o)", p=P))
+            nc.sync.dma_start(weights[:, 1, 0:2], sp.rearrange("(h p) o -> p (h o)", p=P))
+
+        def half(lst, h):
+            return lst[:, h * (H // 16) : (h + 1) * (H // 16)]
+
+        def first_stage(name, h, tab, plane, lst, word_dt, mx_dt, row):
+            words = sbuf(f"{name}_words{h}", [P, H], word_dt)
+            scales = sbuf(f"{name}_scales{h}", [P, H], U8)
+            nc.vector.tensor_copy(scales[:], plane[:].indirect(half(lst, h)))
+            nc.vector.tensor_copy(words[:], tab[:].indirect(half(lst, h)))
+            acc = ps.tile([P, 4, H], F32, name=f"{name}_acc{h}")
+            for t in range(4):
+                cols = slice(t * P, (t + 1) * P)
+                nc.tensor.matmul_mx(
+                    acc[:, t, :], lhsT=w_tab[:, cols].bitcast(E4M3), lhsT_scale=w_plane[:, cols],
+                    rhs=words[:].bitcast(mx_dt), rhs_scale=scales[row:P], start=True, stop=True,
+                )
+            return acc
+
+        a_sb = []
+        for h in range(2):
+            acc = first_stage("a", h, xt_tab, xt_plane, l1, U16, E2M1, 0)
+            a_h = sbuf(f"a_sb{h}", [P, H, 4], F32)
+            nc.scalar.copy(a_h[:], acc[:].rearrange("p t j -> p j t"))
+            a_sb.append(a_h)
+        b_ps = [first_stage("b", h, xo_tab, xo_plane, l2, U32, E4M3, XO_ROW) for h in range(2)]
+
+        nc.vector.tensor_copy(bc_stage[64:128, 0, :].bitcast(I32), bc_stage[0:64, 1, :].bitcast(I32))
+
+        hid = []
+        for h in range(2):
+            hid_h = sbuf(f"hid{h}", [P, H, 4], BF16)
+            nc.vector.tensor_tensor(hid_h[:], b_ps[h][:].rearrange("p t j -> p j t"), a_sb[h][:], MAX)
+            hid.append(hid_h)
+
+        second = [ps.tile([P, J], F32, name=f"second{i}") for i in range(4)]
+        for h in range(2):
+            codes = sbuf(f"hid_codes{h}", [P, H], U32)
+            plane = sbuf(f"hid_plane{h}", [P, H], U8)
+            nc.vector.quantize_mx(codes[:].bitcast(E5M2), plane[:], hid[h][:].rearrange("p j t -> p (j t)"))
+            for g in range(2):
+                nc.tensor.matmul_mx(
+                    second[2 * g][:, h * H : (h + 1) * H],
+                    lhsT=wb_tab[:, g * P // 2 : (g + 1) * P // 2].bitcast(E2M1),
+                    lhsT_scale=bc_stage[:, 0, g * P : (g + 1) * P],
+                    rhs=codes[:].bitcast(E5M2), rhs_scale=plane[:], start=True, stop=True,
+                )
+                nc.tensor.matmul_mx(
+                    second[2 * g + 1][:, h * H : (h + 1) * H],
+                    lhsT=wc_tab[:, g * P : (g + 1) * P].bitcast(E5M2),
+                    lhsT_scale=bc_stage[:, 0, N + g * P : N + (g + 1) * P],
+                    rhs=codes[:].bitcast(E5M2), rhs_scale=plane[:], start=True, stop=True,
+                )
+
+        picked = []
+        for i in range(4):
+            g = i // 2
+            rows = sbuf(f"rows{i}", [P, J], F32)
+            nc.vector.tensor_copy(rows[:], second[i][:])
+            pick = sbuf(f"pick{i}", [P, O], F32)
+            lst = (l3, l4)[i % 2]
+            nc.scalar.activation(pick[:], rows[:].indirect(lst[:]), COPY, scale=weights[:, i % 2, g : g + 1])
+            picked.append(pick)
+        for g in range(2):
+            y = sbuf(f"y{g}", [P, O], F32)
+            nc.vector.tensor_tensor(y[:], picked[2 * g][:], picked[2 * g + 1][:], MAX)
+            nc.sync.dma_start(out[g * P : (g + 1) * P, :], y[:])

@@ -64,16 +64,16 @@ def tile_list_outcomesweighed_oneforboth_kernel(
             return words[0].rearrange("p n t -> p (n t)").bitcast(I32)
 
         nc.sync.dma_start(l1[:], offs)
+        nc.gpsimd.dma_start(xo_tab[:].bitcast(I32), words32(xo_words))
         nc.sync.dma_start(xt_tab[:].bitcast(I32), xt_words[0].bitcast(I32))
         nc.sync.dma_start(w_raw[:].bitcast(I32), words32(w_words))
         nc.scalar.dma_start(w_stage[0:4].bitcast(I32), paired(w_scales)[0])
         nc.scalar.dma_start(w_stage[32:36].bitcast(I32), paired(w_scales)[1])
         nc.scalar.dma_start(xt_stage[64:68].bitcast(I32), paired(xt_scales)[0])
         nc.scalar.dma_start(xt_stage[96:100].bitcast(I32), paired(xt_scales)[1])
-        nc.sync.dma_start(xo_tab[:].bitcast(I32), words32(xo_words))
-        nc.sync.dma_start(l2[:], offs2)
         nc.sync.dma_start(xo_plane[4:8].bitcast(I32), xo_scales[0, 0:4].bitcast(I32))
         nc.sync.dma_start(xo_plane[36:40].bitcast(I32), xo_scales[0, 4:8].bitcast(I32))
+        nc.sync.dma_start(l2[:], offs2)
         nc.sync.dma_start(xo_plane[68:72].bitcast(I32), xo_scales[0, 8:12].bitcast(I32))
         nc.sync.dma_start(xo_plane[100:104].bitcast(I32), xo_scales[0, 12:16].bitcast(I32))
 
@@ -128,11 +128,13 @@ def tile_list_outcomesweighed_oneforboth_kernel(
             a_sb.append(a_h)
         b_ps = [first_stage("b", h, xo_tab, xo_plane, l2, U32, E4M3, XO_ROW) for h in range(2)]
 
-        nc.vector.tensor_copy(bc_stage[64:128, 0, :].bitcast(I32), bc_stage[0:64, 1, :].bitcast(I32))
+        bc_plane = sbuf("bc_plane", [P, 2 * N], U8)
+        nc.vector.tensor_copy(bc_plane[0:64].bitcast(I32), bc_stage[0:64, 0, :].bitcast(I32))
+        nc.vector.tensor_copy(bc_plane[64:128].bitcast(I32), bc_stage[0:64, 1, :].bitcast(I32))
 
         hid = []
         for h in range(2):
-            hid_h = sbuf(f"hid{h}", [P, H, 4], BF16)
+            hid_h = sbuf(f"hid{h}", [P, H, 4], BF16, tag=("bc_stage", "hid1")[h])
             nc.vector.tensor_tensor(hid_h[:], b_ps[h][:].rearrange("p t j -> p j t"), a_sb[h][:], MAX)
             hid.append(hid_h)
 
@@ -145,13 +147,13 @@ def tile_list_outcomesweighed_oneforboth_kernel(
                 nc.tensor.matmul_mx(
                     second[2 * g][:, h * H : (h + 1) * H],
                     lhsT=wb_tab[:, g * P // 2 : (g + 1) * P // 2].bitcast(E2M1),
-                    lhsT_scale=bc_stage[:, 0, g * P : (g + 1) * P],
+                    lhsT_scale=bc_plane[:, g * P : (g + 1) * P],
                     rhs=codes[:].bitcast(E5M2), rhs_scale=plane[:], start=True, stop=True,
                 )
                 nc.tensor.matmul_mx(
                     second[2 * g + 1][:, h * H : (h + 1) * H],
                     lhsT=wc_tab[:, g * P : (g + 1) * P].bitcast(E5M2),
-                    lhsT_scale=bc_stage[:, 0, N + g * P : N + (g + 1) * P],
+                    lhsT_scale=bc_plane[:, N + g * P : N + (g + 1) * P],
                     rhs=codes[:].bitcast(E5M2), rhs_scale=plane[:], start=True, stop=True,
                 )
 

@@ -63,23 +63,23 @@ def tile_list_outcomesweighed_oneforboth_kernel(
         def words32(words):
             return words[0].rearrange("p n t -> p (n t)").bitcast(I32)
 
-        nc.sync.dma_start(l1[:], offs)
-        nc.gpsimd.dma_start(xo_tab[:].bitcast(I32), words32(xo_words))
-        nc.sync.dma_start(xt_tab[:].bitcast(I32), xt_words[0].bitcast(I32))
         nc.sync.dma_start(w_raw[:].bitcast(I32), words32(w_words))
+        nc.gpsimd.dma_start(xo_tab[:].bitcast(I32), words32(xo_words))
         nc.scalar.dma_start(w_stage[0:4].bitcast(I32), paired(w_scales)[0])
-        nc.scalar.dma_start(w_stage[32:36].bitcast(I32), paired(w_scales)[1])
+        nc.sync.dma_start(w_stage[32:36].bitcast(I32), paired(w_scales)[1])
         nc.scalar.dma_start(xt_stage[64:68].bitcast(I32), paired(xt_scales)[0])
-        nc.scalar.dma_start(xt_stage[96:100].bitcast(I32), paired(xt_scales)[1])
+        nc.sync.dma_start(l1[:], offs)
+        nc.sync.dma_start(xt_stage[96:100].bitcast(I32), paired(xt_scales)[1])
+        nc.sync.dma_start(xt_tab[:].bitcast(I32), xt_words[0].bitcast(I32))
         nc.sync.dma_start(xo_plane[4:8].bitcast(I32), xo_scales[0, 0:4].bitcast(I32))
         nc.sync.dma_start(xo_plane[36:40].bitcast(I32), xo_scales[0, 4:8].bitcast(I32))
-        nc.sync.dma_start(l2[:], offs2)
         nc.sync.dma_start(xo_plane[68:72].bitcast(I32), xo_scales[0, 8:12].bitcast(I32))
         nc.sync.dma_start(xo_plane[100:104].bitcast(I32), xo_scales[0, 12:16].bitcast(I32))
+        nc.sync.dma_start(l2[:], offs2)
 
         nc.vector.tensor_copy(w_stage[64:128, 0, :].bitcast(I32), w_stage[0:64, 1, :].bitcast(I32))
         w_plane = sbuf("w_plane", [P, R], U8)
-        nc.gpsimd.tensor_copy(
+        nc.vector.tensor_copy(
             w_plane[:].rearrange("p (t m) -> p t m", t=4),
             w_stage[:, 0, :].rearrange("p (m t) -> p t m", t=4),
         )
@@ -98,10 +98,10 @@ def tile_list_outcomesweighed_oneforboth_kernel(
         nc.sync.dma_start(wc_tab[:].bitcast(I32), words32(wc_words))
         nc.sync.dma_start(l3[:], offs3)
         nc.sync.dma_start(l4[:], offs4)
-        weights = sbuf("weights", [P, 2, 8], F32)
+        weights = sbuf("weights", [P, 2, 8], F32, tag="w_tab")
         with nc.allow_non_contiguous_dma(reason="one float32 a partition and row block"):
-            nc.sync.dma_start(weights[:, 0, 0:2], so.rearrange("(h p) o -> p (h o)", p=P))
-            nc.sync.dma_start(weights[:, 1, 0:2], sp.rearrange("(h p) o -> p (h o)", p=P))
+            nc.scalar.dma_start(weights[:, 0, 0:2], so.rearrange("(h p) o -> p (h o)", p=P))
+            nc.scalar.dma_start(weights[:, 1, 0:2], sp.rearrange("(h p) o -> p (h o)", p=P))
 
         def half(lst, h):
             return lst[:, h * (H // 16) : (h + 1) * (H // 16)]
@@ -132,30 +132,29 @@ def tile_list_outcomesweighed_oneforboth_kernel(
         nc.vector.tensor_copy(bc_plane[0:64].bitcast(I32), bc_stage[0:64, 0, :].bitcast(I32))
         nc.vector.tensor_copy(bc_plane[64:128].bitcast(I32), bc_stage[0:64, 1, :].bitcast(I32))
 
-        hid = []
+        hid = sbuf("hid", [P, J, 4], BF16, tag="bc_stage")
         for h in range(2):
-            hid_h = sbuf(f"hid{h}", [P, H, 4], BF16, tag=("bc_stage", "hid1")[h])
-            nc.vector.tensor_tensor(hid_h[:], b_ps[h][:].rearrange("p t j -> p j t"), a_sb[h][:], MAX)
-            hid.append(hid_h)
+            nc.vector.tensor_tensor(
+                hid[:, h * H : (h + 1) * H, :], b_ps[h][:].rearrange("p t j -> p j t"), a_sb[h][:], MAX
+            )
+        codes = sbuf("hid_codes", [P, J], U32)
+        plane = sbuf("hid_plane", [P, J], U8)
+        nc.vector.quantize_mx(codes[:].bitcast(E5M2), plane[:], hid[:].rearrange("p j t -> p (j t)"))
 
         second = [ps.tile([P, J], F32, name=f"second{i}") for i in range(4)]
-        for h in range(2):
-            codes = sbuf(f"hid_codes{h}", [P, H], U32)
-            plane = sbuf(f"hid_plane{h}", [P, H], U8)
-            nc.vector.quantize_mx(codes[:].bitcast(E5M2), plane[:], hid[h][:].rearrange("p j t -> p (j t)"))
-            for g in range(2):
-                nc.tensor.matmul_mx(
-                    second[2 * g][:, h * H : (h + 1) * H],
-                    lhsT=wb_tab[:, g * P // 2 : (g + 1) * P // 2].bitcast(E2M1),
-                    lhsT_scale=bc_plane[:, g * P : (g + 1) * P],
-                    rhs=codes[:].bitcast(E5M2), rhs_scale=plane[:], start=True, stop=True,
-                )
-                nc.tensor.matmul_mx(
-                    second[2 * g + 1][:, h * H : (h + 1) * H],
-                    lhsT=wc_tab[:, g * P : (g + 1) * P].bitcast(E5M2),
-                    lhsT_scale=bc_plane[:, N + g * P : N + (g + 1) * P],
-                    rhs=codes[:].bitcast(E5M2), rhs_scale=plane[:], start=True, stop=True,
-                )
+        for g in range(2):
+            nc.tensor.matmul_mx(
+                second[2 * g][:],
+                lhsT=wb_tab[:, g * P // 2 : (g + 1) * P // 2].bitcast(E2M1),
+                lhsT_scale=bc_plane[:, g * P : (g + 1) * P],
+                rhs=codes[:].bitcast(E5M2), rhs_scale=plane[:], start=True, stop=True,
+            )
+            nc.tensor.matmul_mx(
+                second[2 * g + 1][:],
+                lhsT=wc_tab[:, g * P : (g + 1) * P].bitcast(E5M2),
+                lhsT_scale=bc_plane[:, N + g * P : N + (g + 1) * P],
+                rhs=codes[:].bitcast(E5M2), rhs_scale=plane[:], start=True, stop=True,
+            )
 
         picked = []
         for i in range(4):

@@ -18,7 +18,9 @@ COPY = mybir.ActivationFunctionType.Copy
 MAX = mybir.AluOpType.max
 
 P = 128
-H = 128
+PACK = 4
+PER_COLUMN = 16
+H = J // 2
 XO_ROW = 4
 
 
@@ -34,10 +36,10 @@ def tile_list_outcomesweighed_oneforboth_kernel(
         def sbuf(name, shape, dtype, tag=None):
             return sb.tile(shape, dtype, name=name, tag=tag or name, align_bytes=64)
 
-        l1 = sbuf("l1", [P, J // 16], U16)
-        l2 = sbuf("l2", [P, J // 16], U16)
-        l3 = sbuf("l3", [P, O // 16], U16)
-        l4 = sbuf("l4", [P, O // 16], U16)
+        list1 = sbuf("list1", [P, J // PER_COLUMN], U16)
+        list2 = sbuf("list2", [P, J // PER_COLUMN], U16)
+        list3 = sbuf("list3", [P, O // PER_COLUMN], U16)
+        list4 = sbuf("list4", [P, O // PER_COLUMN], U16)
         xt_tab = sbuf("xt_tab", [P, T], U16)
         xo_tab = sbuf("xo_tab", [P, Z], U32)
         w_raw = sbuf("w_raw", [P, R], U32)
@@ -49,8 +51,8 @@ def tile_list_outcomesweighed_oneforboth_kernel(
         wb_tab = sbuf("wb_tab", [P, N // 2], U32)
         wc_tab = sbuf("wc_tab", [P, N], U32)
 
-        def flat32(t):
-            return t[:].rearrange("p a c -> p (a c)").bitcast(I32)
+        def flat32(stage):
+            return stage[:].rearrange("p a c -> p (a c)").bitcast(I32)
 
         nc.vector.memset(flat32(w_stage)[0:64], 0)
         nc.vector.memset(flat32(xt_stage)[64:128], 0)
@@ -58,7 +60,7 @@ def tile_list_outcomesweighed_oneforboth_kernel(
         nc.vector.memset(flat32(bc_stage)[0:64], 0)
 
         def paired(scales):
-            return scales[0].bitcast(I32).rearrange("(a b r) c -> b r a c", a=2, b=2)
+            return scales[0].bitcast(I32).rearrange("(a b i) c -> b i a c", a=2, b=2)
 
         def words32(words):
             return words[0].rearrange("p n t -> p (n t)").bitcast(I32)
@@ -68,104 +70,110 @@ def tile_list_outcomesweighed_oneforboth_kernel(
         nc.scalar.dma_start(w_stage[0:4].bitcast(I32), paired(w_scales)[0])
         nc.sync.dma_start(w_stage[32:36].bitcast(I32), paired(w_scales)[1])
         nc.scalar.dma_start(xt_stage[64:68].bitcast(I32), paired(xt_scales)[0])
-        nc.sync.dma_start(l1[:], offs)
+        nc.sync.dma_start(list1[:], offs)
         nc.sync.dma_start(xt_stage[96:100].bitcast(I32), paired(xt_scales)[1])
         nc.sync.dma_start(xt_tab[:].bitcast(I32), xt_words[0].bitcast(I32))
-        nc.sync.dma_start(xo_plane[4:8].bitcast(I32), xo_scales[0, 0:4].bitcast(I32))
-        nc.sync.dma_start(xo_plane[36:40].bitcast(I32), xo_scales[0, 4:8].bitcast(I32))
-        nc.sync.dma_start(xo_plane[68:72].bitcast(I32), xo_scales[0, 8:12].bitcast(I32))
-        nc.sync.dma_start(xo_plane[100:104].bitcast(I32), xo_scales[0, 12:16].bitcast(I32))
-        nc.sync.dma_start(l2[:], offs2)
+        for quadrant in range(4):
+            first = 32 * quadrant + XO_ROW
+            nc.sync.dma_start(
+                xo_plane[first : first + PACK].bitcast(I32),
+                xo_scales[0, PACK * quadrant : PACK * (quadrant + 1)].bitcast(I32),
+            )
+        nc.sync.dma_start(list2[:], offs2)
 
         nc.vector.tensor_copy(w_stage[64:128, 0, :].bitcast(I32), w_stage[0:64, 1, :].bitcast(I32))
-        w_plane = sbuf("w_plane", [P, R], U8)
-        nc.vector.tensor_copy(
-            w_plane[:].rearrange("p (t m) -> p t m", t=4),
-            w_stage[:, 0, :].rearrange("p (m t) -> p t m", t=4),
-        )
         w_tab = sbuf("w_tab", [P, R], U32)
         nc.scalar.copy(
-            w_tab[:].rearrange("p (t c i) -> p c t i", t=4, i=4),
-            w_raw[:].rearrange("p (c i t) -> p c t i", t=4, i=4),
+            w_tab[:].rearrange("p (t c i) -> p c t i", t=PACK, i=4),
+            w_raw[:].rearrange("p (c i t) -> p c t i", t=PACK, i=4),
         )
         nc.vector.tensor_copy(xt_plane[64:128].bitcast(I32), xt_stage[64:128, 1, :].bitcast(I32))
         nc.vector.tensor_copy(xt_plane[0:64].bitcast(I32), xt_stage[64:128, 0, :].bitcast(I32))
+        w_plane = sbuf("w_plane", [P, R], U8, tag="xt_stage")
+        nc.vector.tensor_copy(
+            w_plane[:].rearrange("p (t m) -> p t m", t=PACK),
+            w_stage[:, 0, :].rearrange("p (m t) -> p t m", t=PACK),
+        )
 
-        for b in range(2):
-            nc.sync.dma_start(bc_stage[32 * b : 32 * b + 4, :, 0:N].bitcast(I32), paired(wb_scales)[b])
-            nc.sync.dma_start(bc_stage[32 * b : 32 * b + 4, :, N : 2 * N].bitcast(I32), paired(wc_scales)[b])
+        for quadrant in range(2):
+            rows = slice(32 * quadrant, 32 * quadrant + PACK)
+            nc.sync.dma_start(bc_stage[rows, :, 0:N].bitcast(I32), paired(wb_scales)[quadrant])
+            nc.sync.dma_start(bc_stage[rows, :, N : 2 * N].bitcast(I32), paired(wc_scales)[quadrant])
         nc.sync.dma_start(wb_tab[:].bitcast(I32), wb_words[0].bitcast(I32))
         nc.sync.dma_start(wc_tab[:].bitcast(I32), words32(wc_words))
-        nc.sync.dma_start(l3[:], offs3)
-        nc.sync.dma_start(l4[:], offs4)
+        nc.sync.dma_start(list3[:], offs3)
+        nc.sync.dma_start(list4[:], offs4)
         weights = sbuf("weights", [P, 2, 8], F32, tag="w_tab")
-        with nc.allow_non_contiguous_dma(reason="one float32 a partition and row block"):
-            nc.scalar.dma_start(weights[:, 0, 0:2], so.rearrange("(h p) o -> p (h o)", p=P))
-            nc.scalar.dma_start(weights[:, 1, 0:2], sp.rearrange("(h p) o -> p (h o)", p=P))
+        with nc.allow_non_contiguous_dma(reason="one float32 a partition and block of 128 output rows"):
+            nc.scalar.dma_start(weights[:, 0, 0:2], so.rearrange("(g p) o -> p (g o)", p=P))
+            nc.scalar.dma_start(weights[:, 1, 0:2], sp.rearrange("(g p) o -> p (g o)", p=P))
 
-        def half(lst, h):
-            return lst[:, h * (H // 16) : (h + 1) * (H // 16)]
-
-        def first_stage(name, h, tab, plane, lst, word_dt, mx_dt, row):
-            words = sbuf(f"{name}_words{h}", [P, H], word_dt)
+        def first_stage(name, h, tab, plane, offsets, word_dtype, mx_dtype, row):
+            entries = offsets[:, h * (H // PER_COLUMN) : (h + 1) * (H // PER_COLUMN)]
+            words = sbuf(f"{name}_words{h}", [P, H], word_dtype)
             scales = sbuf(f"{name}_scales{h}", [P, H], U8)
-            nc.vector.tensor_copy(scales[:], plane[:].indirect(half(lst, h)))
-            nc.vector.tensor_copy(words[:], tab[:].indirect(half(lst, h)))
-            acc = ps.tile([P, 4, H], F32, name=f"{name}_acc{h}")
-            for t in range(4):
+            nc.vector.tensor_copy(scales[:], plane[:].indirect(entries))
+            nc.vector.tensor_copy(words[:], tab[:].indirect(entries))
+            acc = ps.tile([P, PACK, H], F32, name=f"{name}_acc{h}")
+            for t in range(PACK):
                 cols = slice(t * P, (t + 1) * P)
                 nc.tensor.matmul_mx(
                     acc[:, t, :], lhsT=w_tab[:, cols].bitcast(E4M3), lhsT_scale=w_plane[:, cols],
-                    rhs=words[:].bitcast(mx_dt), rhs_scale=scales[row:P], start=True, stop=True,
+                    rhs=words[:].bitcast(mx_dtype), rhs_scale=scales[row:P], start=True, stop=True,
                 )
             return acc
 
         a_sb = []
         for h in range(2):
-            acc = first_stage("a", h, xt_tab, xt_plane, l1, U16, E2M1, 0)
-            a_h = sbuf(f"a_sb{h}", [P, H, 4], F32)
-            nc.scalar.copy(a_h[:], acc[:].rearrange("p t j -> p j t"))
-            a_sb.append(a_h)
-        b_ps = [first_stage("b", h, xo_tab, xo_plane, l2, U32, E4M3, XO_ROW) for h in range(2)]
+            acc = first_stage("a", h, xt_tab, xt_plane, list1, U16, E2M1, 0)
+            a_half = sbuf(f"a_sb{h}", [P, H, PACK], F32)
+            nc.scalar.copy(a_half[:], acc[:].rearrange("p t j -> p j t"))
+            a_sb.append(a_half)
+        b_ps = [first_stage("b", h, xo_tab, xo_plane, list2, U32, E4M3, XO_ROW) for h in range(2)]
 
         bc_plane = sbuf("bc_plane", [P, 2 * N], U8)
         nc.vector.tensor_copy(bc_plane[0:64].bitcast(I32), bc_stage[0:64, 0, :].bitcast(I32))
         nc.vector.tensor_copy(bc_plane[64:128].bitcast(I32), bc_stage[0:64, 1, :].bitcast(I32))
 
-        hid = sbuf("hid", [P, J, 4], BF16, tag="bc_stage")
+        hid = sbuf("hid", [P, J, PACK], BF16, tag="bc_stage")
         for h in range(2):
             nc.vector.tensor_tensor(
                 hid[:, h * H : (h + 1) * H, :], b_ps[h][:].rearrange("p t j -> p j t"), a_sb[h][:], MAX
             )
-        codes = sbuf("hid_codes", [P, J], U32)
-        plane = sbuf("hid_plane", [P, J], U8)
-        nc.vector.quantize_mx(codes[:].bitcast(E5M2), plane[:], hid[:].rearrange("p j t -> p (j t)"))
+        hid_words = [sbuf(f"hid_words{h}", [P, H], U32) for h in range(2)]
+        hid_plane = [sbuf(f"hid_plane{h}", [P, H], U8) for h in range(2)]
+        for h in range(2):
+            nc.vector.quantize_mx(
+                hid_words[h][:].bitcast(E5M2), hid_plane[h][:],
+                hid[:, h * H : (h + 1) * H, :].rearrange("p j t -> p (j t)"),
+            )
 
         second = [ps.tile([P, J], F32, name=f"second{i}") for i in range(4)]
-        for g in range(2):
-            nc.tensor.matmul_mx(
-                second[2 * g][:],
-                lhsT=wb_tab[:, g * P // 2 : (g + 1) * P // 2].bitcast(E2M1),
-                lhsT_scale=bc_plane[:, g * P : (g + 1) * P],
-                rhs=codes[:].bitcast(E5M2), rhs_scale=plane[:], start=True, stop=True,
-            )
-            nc.tensor.matmul_mx(
-                second[2 * g + 1][:],
-                lhsT=wc_tab[:, g * P : (g + 1) * P].bitcast(E5M2),
-                lhsT_scale=bc_plane[:, N + g * P : N + (g + 1) * P],
-                rhs=codes[:].bitcast(E5M2), rhs_scale=plane[:], start=True, stop=True,
-            )
+        for i in range(4):
+            g, which = divmod(i, 2)
+            stationary = (
+                wb_tab[:, g * P // 2 : (g + 1) * P // 2].bitcast(E2M1),
+                wc_tab[:, g * P : (g + 1) * P].bitcast(E5M2),
+            )[which]
+            for h in range(2):
+                nc.tensor.matmul_mx(
+                    second[i][:, h * H : (h + 1) * H], lhsT=stationary,
+                    lhsT_scale=bc_plane[:, which * N + g * P : which * N + (g + 1) * P],
+                    rhs=hid_words[h][:].bitcast(E5M2), rhs_scale=hid_plane[h][:], start=True, stop=True,
+                )
 
         picked = []
         for i in range(4):
-            g = i // 2
-            rows = sbuf(f"rows{i}", [P, J], F32)
-            nc.vector.tensor_copy(rows[:], second[i][:])
+            g, which = divmod(i, 2)
+            outcome = sbuf(f"outcome{i}", [P, J], F32)
+            nc.vector.tensor_copy(outcome[:], second[i][:])
             pick = sbuf(f"pick{i}", [P, O], F32)
-            lst = (l3, l4)[i % 2]
-            nc.scalar.activation(pick[:], rows[:].indirect(lst[:]), COPY, scale=weights[:, i % 2, g : g + 1])
+            offsets = (list3, list4)[which]
+            nc.scalar.activation(
+                pick[:], outcome[:].indirect(offsets[:]), COPY, scale=weights[:, which, g : g + 1]
+            )
             picked.append(pick)
         for g in range(2):
-            y = sbuf(f"y{g}", [P, O], F32)
-            nc.vector.tensor_tensor(y[:], picked[2 * g][:], picked[2 * g + 1][:], MAX)
-            nc.sync.dma_start(out[g * P : (g + 1) * P, :], y[:])
+            larger = sbuf(f"larger{g}", [P, O], F32)
+            nc.vector.tensor_tensor(larger[:], picked[2 * g][:], picked[2 * g + 1][:], MAX)
+            nc.sync.dma_start(out[g * P : (g + 1) * P, :], larger[:])

from contextlib import ExitStack

import concourse.mybir as mybir

K, T, Z, J, R, N, O = 512, 1024, 1024, 256, 512, 256, 128
FLOPS = 2 * (2 * K * R * J + 2 * R * N * J)

F32 = mybir.dt.float32
BF16 = mybir.dt.bfloat16
I32 = mybir.dt.int32
U32 = mybir.dt.uint32
U16 = mybir.dt.uint16
U8 = mybir.dt.uint8
E4M3 = mybir.dt.float8_e4m3fn_x4
E5M2 = mybir.dt.float8_e5m2_x4
E2M1 = mybir.dt.float4_e2m1fn_x4
COPY = mybir.ActivationFunctionType.Copy
MAX = mybir.AluOpType.max

P = 128
PACK = 4
PER_COLUMN = 16
H = J // 2
XO_ROW = 4


def tile_list_outcomesweighed_oneforboth_kernel(
    tc, xt_words, xt_scales, xo_words, xo_scales, w_words, w_scales, wb_words, wb_scales,
    wc_words, wc_scales, so, sp, offs, offs2, offs3, offs4, out,
):
    nc = tc.nc
    with ExitStack() as ctx:
        sb = ctx.enter_context(tc.tile_pool(name="sb", bufs=1))
        ps = ctx.enter_context(tc.psum_pool(name="ps", bufs=1))

        def sbuf(name, shape, dtype, tag=None):
            return sb.tile(shape, dtype, name=name, tag=tag or name, align_bytes=64)

        list1 = sbuf("list1", [P, J // PER_COLUMN], U16)
        list2 = sbuf("list2", [P, J // PER_COLUMN], U16)
        list3 = sbuf("list3", [P, O // PER_COLUMN], U16)
        list4 = sbuf("list4", [P, O // PER_COLUMN], U16)
        xt_tab = sbuf("xt_tab", [P, T], U16)
        xo_tab = sbuf("xo_tab", [P, Z], U32)
        w_raw = sbuf("w_raw", [P, R], U32)
        xt_stage = sbuf("xt_stage", [P, 2, T], U8)
        xt_plane = sbuf("xt_plane", [P, T], U8)
        xo_plane = sbuf("xo_plane", [P, Z], U8)
        w_stage = sbuf("w_stage", [P, 2, R], U8)
        bc_stage = sbuf("bc_stage", [P, 2, 2 * N], U8)
        wb_tab = sbuf("wb_tab", [P, N // 2], U32)
        wc_tab = sbuf("wc_tab", [P, N], U32)

        def flat32(stage):
            return stage[:].rearrange("p a c -> p (a c)").bitcast(I32)

        nc.vector.memset(flat32(w_stage)[0:64], 0)
        nc.vector.memset(flat32(xt_stage)[64:128], 0)
        nc.vector.memset(xo_plane[:].bitcast(I32), 0)
        nc.vector.memset(flat32(bc_stage)[0:64], 0)

        def paired(scales):
            return scales[0].bitcast(I32).rearrange("(a b i) c -> b i a c", a=2, b=2)

        def words32(words):
            return words[0].rearrange("p n t -> p (n t)").bitcast(I32)

        nc.sync.dma_start(w_raw[:].bitcast(I32), words32(w_words))
        nc.gpsimd.dma_start(xo_tab[:].bitcast(I32), words32(xo_words))
        nc.scalar.dma_start(w_stage[0:4].bitcast(I32), paired(w_scales)[0])
        nc.sync.dma_start(w_stage[32:36].bitcast(I32), paired(w_scales)[1])
        nc.scalar.dma_start(xt_stage[64:68].bitcast(I32), paired(xt_scales)[0])
        nc.sync.dma_start(list1[:], offs)
        nc.sync.dma_start(xt_stage[96:100].bitcast(I32), paired(xt_scales)[1])
        nc.sync.dma_start(xt_tab[:].bitcast(I32), xt_words[0].bitcast(I32))
        for quadrant in range(4):
            first = 32 * quadrant + XO_ROW
            nc.sync.dma_start(
                xo_plane[first : first + PACK].bitcast(I32),
                xo_scales[0, PACK * quadrant : PACK * (quadrant + 1)].bitcast(I32),
            )
        nc.sync.dma_start(list2[:], offs2)

        nc.vector.tensor_copy(w_stage[64:128, 0, :].bitcast(I32), w_stage[0:64, 1, :].bitcast(I32))
        w_tab = sbuf("w_tab", [P, R], U32)
        nc.scalar.copy(
            w_tab[:].rearrange("p (t c i) -> p c t i", t=PACK, i=4),
            w_raw[:].rearrange("p (c i t) -> p c t i", t=PACK, i=4),
        )
        nc.vector.tensor_copy(xt_plane[64:128].bitcast(I32), xt_stage[64:128, 1, :].bitcast(I32))
        nc.vector.tensor_copy(xt_plane[0:64].bitcast(I32), xt_stage[64:128, 0, :].bitcast(I32))
        w_plane = sbuf("w_plane", [P, R], U8, tag="xt_stage")
        nc.vector.tensor_copy(
            w_plane[:].rearrange("p (t m) -> p t m", t=PACK),
            w_stage[:, 0, :].rearrange("p (m t) -> p t m", t=PACK),
        )

        for quadrant in range(2):
            rows = slice(32 * quadrant, 32 * quadrant + PACK)
            nc.sync.dma_start(bc_stage[rows, :, 0:N].bitcast(I32), paired(wb_scales)[quadrant])
            nc.sync.dma_start(bc_stage[rows, :, N : 2 * N].bitcast(I32), paired(wc_scales)[quadrant])
        nc.sync.dma_start(wb_tab[:].bitcast(I32), wb_words[0].bitcast(I32))
        nc.sync.dma_start(wc_tab[:].bitcast(I32), words32(wc_words))
        nc.sync.dma_start(list3[:], offs3)
        nc.sync.dma_start(list4[:], offs4)
        weights = sbuf("weights", [P, 2, 8], F32, tag="w_tab")
        with nc.allow_non_contiguous_dma(reason="one float32 a partition and block of 128 output rows"):
            nc.scalar.dma_start(weights[:, 0, 0:2], so.rearrange("(g p) o -> p (g o)", p=P))
            nc.scalar.dma_start(weights[:, 1, 0:2], sp.rearrange("(g p) o -> p (g o)", p=P))

        def first_stage(name, h, tab, plane, offsets, word_dtype, mx_dtype, row):
            entries = offsets[:, h * (H // PER_COLUMN) : (h + 1) * (H // PER_COLUMN)]
            words = sbuf(f"{name}_words{h}", [P, H], word_dtype)
            scales = sbuf(f"{name}_scales{h}", [P, H], U8)
            nc.vector.tensor_copy(scales[:], plane[:].indirect(entries))
            nc.vector.tensor_copy(words[:], tab[:].indirect(entries))
            acc = ps.tile([P, PACK, H], F32, name=f"{name}_acc{h}")
            for t in range(PACK):
                cols = slice(t * P, (t + 1) * P)
                nc.tensor.matmul_mx(
                    acc[:, t, :], lhsT=w_tab[:, cols].bitcast(E4M3), lhsT_scale=w_plane[:, cols],
                    rhs=words[:].bitcast(mx_dtype), rhs_scale=scales[row:P], start=True, stop=True,
                )
            return acc

        a_sb = []
        for h in range(2):
            acc = first_stage("a", h, xt_tab, xt_plane, list1, U16, E2M1, 0)
            a_half = sbuf(f"a_sb{h}", [P, H, PACK], F32)
            nc.scalar.copy(a_half[:], acc[:].rearrange("p t j -> p j t"))
            a_sb.append(a_half)
        b_ps = [first_stage("b", h, xo_tab, xo_plane, list2, U32, E4M3, XO_ROW) for h in range(2)]

        bc_plane = sbuf("bc_plane", [P, 2 * N], U8)
        nc.vector.tensor_copy(bc_plane[0:64].bitcast(I32), bc_stage[0:64, 0, :].bitcast(I32))
        nc.vector.tensor_copy(bc_plane[64:128].bitcast(I32), bc_stage[0:64, 1, :].bitcast(I32))

        hid = sbuf("hid", [P, J, PACK], BF16, tag="bc_stage")
        for h in range(2):
            nc.vector.tensor_tensor(
                hid[:, h * H : (h + 1) * H, :], b_ps[h][:].rearrange("p t j -> p j t"), a_sb[h][:], MAX
            )
        hid_words = [sbuf(f"hid_words{h}", [P, H], U32) for h in range(2)]
        hid_plane = [sbuf(f"hid_plane{h}", [P, H], U8) for h in range(2)]
        for h in range(2):
            nc.vector.quantize_mx(
                hid_words[h][:].bitcast(E5M2), hid_plane[h][:],
                hid[:, h * H : (h + 1) * H, :].rearrange("p j t -> p (j t)"),
            )

        second = [ps.tile([P, J], F32, name=f"second{i}") for i in range(4)]
        for i in range(4):
            g, which = divmod(i, 2)
            stationary = (
                wb_tab[:, g * P // 2 : (g + 1) * P // 2].bitcast(E2M1),
                wc_tab[:, g * P : (g + 1) * P].bitcast(E5M2),
            )[which]
            for h in range(2):
                nc.tensor.matmul_mx(
                    second[i][:, h * H : (h + 1) * H], lhsT=stationary,
                    lhsT_scale=bc_plane[:, which * N + g * P : which * N + (g + 1) * P],
                    rhs=hid_words[h][:].bitcast(E5M2), rhs_scale=hid_plane[h][:], start=True, stop=True,
                )

        picked = []
        for i in range(4):
            g, which = divmod(i, 2)
            outcome = sbuf(f"outcome{i}", [P, J], F32)
            nc.vector.tensor_copy(outcome[:], second[i][:])
            pick = sbuf(f"pick{i}", [P, O], F32)
            offsets = (list3, list4)[which]
            nc.scalar.activation(
                pick[:], outcome[:].indirect(offsets[:]), COPY, scale=weights[:, which, g : g + 1]
            )
            picked.append(pick)
        for g in range(2):
            larger = sbuf(f"larger{g}", [P, O], F32)
            nc.vector.tensor_tensor(larger[:], picked[2 * g][:], picked[2 * g + 1][:], MAX)
            nc.sync.dma_start(out[g * P : (g + 1) * P, :], larger[:])
